import numpy as np
import ml_dtypes


def mxq(x, axis, fmt="e4m3"):
    dtype, down = {"e4m3": (ml_dtypes.float8_e4m3fn, 7), "e5m2": (ml_dtypes.float8_e5m2, 14)}[fmt]
    v = np.moveaxis(np.asarray(x, np.float32).astype(ml_dtypes.bfloat16).astype(np.float64), axis, -1)
    blocks = v.reshape(v.shape[:-1] + (-1, 32))
    amax = np.abs(blocks).max(-1, keepdims=True)
    byte = np.maximum(np.where(amax > 0, np.frexp(amax)[1] - 1 + 127, 0) - down, 1)
    scale = np.exp2(byte - 127.0)
    codes = (blocks / scale).astype(np.float32).astype(dtype).astype(np.float64)
    return np.moveaxis((codes * scale).reshape(v.shape), -1, axis)


WIDE = False


def mx_kscale(k):
    if not WIDE:
        return np.ones(k)
    levels = np.array([10, -10, 5, -5, 0])
    if k % 512:
        return np.exp2(np.random.permutation(np.resize(levels, k // 32))).repeat(32)
    a = np.empty((k // 512, 16))
    for p in range(k // 512):
        a[p, :8] = np.random.permutation(np.resize(levels, 8))
        for g in range(8):
            far = levels[np.abs(levels - a[p, g]) >= 10]
            a[p, g + 8] = far[np.random.randint(len(far))]
    return np.exp2(a.ravel()).repeat(32)


def f64(x):
    return np.asarray(x).astype(np.float64)


def striped8(idx):
    return np.asarray(idx).reshape(8, -1, 16).transpose(0, 2, 1).reshape(128, -1).astype(np.uint16)


def unstriped8(offs):
    return offs.reshape(8, 16, -1).transpose(0, 2, 1).reshape(8, -1).astype(np.int64)


def pick8(x, idx, run):
    r = np.arange(len(x))
    return x[r[:, None], idx[r % (8 * run) // run]]


E2M1 = np.array([0.0, 0.5, 1.0, 1.5, 2.0, 3.0, 4.0, 6.0, -0.0, -0.5, -1.0, -1.5, -2.0, -3.0, -4.0, -6.0])


def pack_weight(w, fmt):
    k, n = w.shape
    w = f64(np.asarray(w, np.float32).astype(ml_dtypes.bfloat16)).reshape(k // 32, 32, n)
    amax = np.abs(w).max(1)
    if fmt == "e4m3":
        byte = np.frexp(amax)[1] - 1 + 127 - 7
    else:
        mant, ex = np.frexp(amax / 6.0)
        byte = np.where(mant > 0.5, ex, ex - 1) + 127
    byte = np.clip(np.where(amax > 0, byte, 1), 1, 254)
    scaled = (w * np.exp2(127.0 - byte)[:, None, :]).reshape(k, n).astype(np.float32)
    by_word = np.ascontiguousarray(scaled.reshape(k // 512, 128, 4, n).transpose(0, 1, 3, 2))
    if fmt == "e4m3":
        words = by_word.astype(ml_dtypes.float8_e4m3fn).view(np.uint8)
    else:
        c = by_word.astype(ml_dtypes.float4_e2m1fn).view(np.uint8) & 0xF
        words = (c[..., 0::2] | (c[..., 1::2] << 4)).reshape(k // 512, 128, 2 * n)
    return np.ascontiguousarray(words), np.ascontiguousarray(byte.astype(np.uint8).reshape(k // 512, 16, n))


def unpack_weight(words, scales, fmt):
    g, _, n = scales.shape
    words = np.ascontiguousarray(words).reshape(g, 128, n, -1)
    if fmt == "e4m3":
        vals = words.view(ml_dtypes.float8_e4m3fn).astype(np.float64)
    else:
        nib = np.empty((g, 128, n, 4), np.uint8)
        nib[..., 0::2] = words & 0xF
        nib[..., 1::2] = words >> 4
        vals = E2M1[nib]
    vals = vals * np.repeat(np.exp2(scales.astype(np.float64) - 127.0), 8, axis=1)[..., None]
    return vals.transpose(0, 1, 3, 2).reshape(g * 512, n)


D, T, U, I, J, Q = 512, 1024, 1024, 512, 256, 128


def setup_inputs():
    n = np.random.standard_normal
    idx = np.stack([np.random.permutation(T)[:I] for _ in range(8)])
    idx2 = np.stack([np.random.permutation(U)[:I] for _ in range(8)])
    idx3 = np.stack([np.random.permutation(T)[:J] for _ in range(8)])
    idx4 = np.stack([np.random.permutation(U)[:J] for _ in range(8)])
    idx5 = np.stack([np.random.permutation(U)[:I] for _ in range(8)])
    fd = mx_kscale(D)
    cachep = pack_weight(n((D, T)) / fd[:, None], "e4m3")
    draftp = pack_weight(n((D, U)) / fd[:, None], "e2m1")
    return {
        "query": (n((D, Q)) * 1.0 / np.sqrt(D) * fd[:, None]).astype(np.float32),
        "cache_words": cachep[0],
        "cache_scales": cachep[1],
        "draft_words": draftp[0],
        "draft_scales": draftp[1],
        "offs": striped8(idx),
        "offs2": striped8(idx2),
        "offs3": striped8(idx3),
        "offs4": striped8(idx4),
        "offs5": striped8(idx5),
    }


def reference(query, cache_words, cache_scales, draft_words, draft_scales, offs, offs2, offs3, offs4, offs5):
    idx = unstriped8(offs)
    idx2 = unstriped8(offs2)
    idx3 = unstriped8(offs3)
    idx4 = unstriped8(offs4)
    idx5 = unstriped8(offs5)
    cacheu = unpack_weight(cache_words, cache_scales, "e4m3")
    draftu = unpack_weight(draft_words, draft_scales, "e2m1")
    queryq = mxq(f64(query), 0, "e4m3")
    a = queryq.T @ cacheu
    b = queryq.T @ draftu
    w = pick8(a, idx, 16) - pick8(b, idx2, 16)
    acc = w[:, 0:0 + J]
    rej = w[:, 256:256 + J]
    f1 = np.zeros((Q, T))
    f1[np.arange(Q)[:, None], idx3[np.arange(Q) % 128 // 16]] = acc
    f2 = np.zeros((Q, U))
    f2[np.arange(Q)[:, None], idx4[np.arange(Q) % 128 // 16]] = rej
    aa = a + f1
    bb = b - f2
    y = np.maximum(pick8(aa, idx, 16), pick8(bb, idx5, 16))
    return y

@@ -1,0 +1,150 @@
+from contextlib import ExitStack
+
+import concourse.mybir as mybir
+
+D, T, I, J, Q = 512, 1024, 512, 256, 128
+FLOPS = 2 * 2 * D * T * Q
+
+F32 = mybir.dt.float32
+BF16 = mybir.dt.bfloat16
+I32 = mybir.dt.int32
+U32 = mybir.dt.uint32
+U16 = mybir.dt.uint16
+U8 = mybir.dt.uint8
+FP8X4 = mybir.dt.float8_e4m3fn_x4
+FP4X4 = mybir.dt.float4_e2m1fn_x4
+ADD = mybir.AluOpType.add
+SUB = mybir.AluOpType.subtract
+MAX = mybir.AluOpType.max
+COPY = mybir.ActivationFunctionType.Copy
+
+P = 128
+PACK = 4
+N = 256
+HALF = J // 16
+
+
+def load_scales(nc, plane, scales):
+    words = plane[:].bitcast(I32)
+    rows = scales[0].bitcast(I32)
+    for first in (0, 64):
+        src = rows[first // 8 : first // 8 + 8, :].rearrange("(s r) c -> r s c", r=4)
+        dst = words[first : first + 4, :].rearrange("p (s c) -> p s c", s=2)
+        nc.sync.dma_start(out=dst, in_=src)
+
+
+def spread_scales(nc, plane):
+    words = plane[:].bitcast(I32)
+    for first in (0, 64):
+        nc.vector.tensor_copy(
+            out=words[first + 32 : first + 36, 0 : T // 4],
+            in_=words[first : first + 4, T // 4 : T // 2],
+        )
+
+
+def leave_psum(nc, on_vector, dst, bank):
+    if on_vector:
+        nc.vector.tensor_copy(out=dst, in_=bank)
+    else:
+        nc.scalar.copy(out=dst, in_=bank)
+
+
+def tile_attend_acceptback_two_kernel(
+    tc, query, cache_words, cache_scales, draft_words, draft_scales, offs, offs2, offs3, offs4, offs5, out
+):
+    nc = tc.nc
+    with ExitStack() as ctx:
+        sb = ctx.enter_context(tc.tile_pool(name="sb", bufs=1))
+        ps = ctx.enter_context(tc.psum_pool(name="ps", bufs=1))
+
+        d_plane = sb.tile([P, 2 * T], U8, align_bytes=64)
+        c_plane = sb.tile([P, 2 * T], U8, align_bytes=64)
+        q_raw = sb.tile([P, PACK, Q], F32)
+        nc.sync.dma_start(out=q_raw[:], in_=query.rearrange("(p j) w -> p j w", j=PACK))
+        load_scales(nc, d_plane, draft_scales)
+        d_codes = sb.tile([P, 2 * T], U8, align_bytes=64)
+        nc.sync.dma_start(out=d_codes[:].bitcast(I32), in_=draft_words[0].bitcast(I32))
+        load_scales(nc, c_plane, cache_scales)
+        c_src = cache_words[0].rearrange("p n t -> p (n t)").bitcast(I32)
+        c_codes = []
+        for h in range(2):
+            part = sb.tile([P, T // 2], I32, align_bytes=64, name="c_codes%d" % h)
+            nc.sync.dma_start(out=part[:], in_=c_src[:, h * (T // 2) : (h + 1) * (T // 2)])
+            c_codes.append(part)
+
+        l2 = sb.tile([P, I // 16], U16)
+        nc.sync.dma_start(l2[:], offs2)
+        l1 = sb.tile([P, I // 16], U16)
+        nc.sync.dma_start(l1[:], offs)
+        l3 = sb.tile([P, J // 16], U16)
+        nc.sync.dma_start(l3[:], offs3)
+        l4 = sb.tile([P, J // 16], U16)
+        nc.sync.dma_start(l4[:], offs4)
+        l5 = sb.tile([P, I // 16], U16)
+        nc.sync.dma_start(l5[:], offs5)
+
+        f1 = sb.tile([P, T], F32)
+        f2 = sb.tile([P, T], F32)
+        nc.vector.memset(f1[:], 0.0)
+        nc.vector.memset(f2[:], 0.0)
+
+        q_bf = sb.tile([P, Q, PACK], BF16, align_bytes=64)
+        nc.vector.tensor_copy(out=q_bf[:], in_=q_raw[:].rearrange("p j w -> p w j"))
+        spread_scales(nc, d_plane)
+        q_codes = sb.tile([P, Q], U32, align_bytes=64)
+        q_plane = sb.tile([P, Q], U8, align_bytes=64)
+        nc.vector.quantize_mx(
+            out=q_codes[:].bitcast(FP8X4), scales=q_plane[:], in_=q_bf[:].rearrange("p w j -> p (w j)")
+        )
+        spread_scales(nc, c_plane)
+
+        a = sb.tile([P, T], F32)
+        b = sb.tile([P, T], F32)
+        for c in range(T // N):
+            bank = ps.tile([P, N], F32, name="b_bank%d" % c)
+            nc.tensor.matmul_mx(
+                out=bank[:],
+                lhsT=q_codes[:].bitcast(FP8X4),
+                lhsT_scale=q_plane[:],
+                rhs=d_codes[:, 2 * c * N : 2 * (c + 1) * N].bitcast(FP4X4),
+                rhs_scale=d_plane[:, c * N : (c + 1) * N],
+                start=True,
+                stop=True,
+            )
+            leave_psum(nc, c % 2 == 1, b[:, c * N : (c + 1) * N], bank[:])
+        for c in range(T // N):
+            bank = ps.tile([P, N], F32, name="a_bank%d" % c)
+            nc.tensor.matmul_mx(
+                out=bank[:],
+                lhsT=q_codes[:].bitcast(FP8X4),
+                lhsT_scale=q_plane[:],
+                rhs=c_codes[c // 2][:, (c % 2) * N : (c % 2 + 1) * N].bitcast(FP8X4),
+                rhs_scale=c_plane[:, c * N : (c + 1) * N],
+                start=True,
+                stop=True,
+            )
+            leave_psum(nc, c == 2, a[:, c * N : (c + 1) * N], bank[:])
+
+        halves = [slice(h * HALF, (h + 1) * HALF) for h in range(2)]
+        lead = [sb.tile([P, J], F32, name="lead%d" % h) for h in range(2)]
+        for h in range(2):
+            b_picked = sb.tile([P, J], F32)
+            nc.vector.tensor_copy(out=b_picked[:], in_=b[:].indirect(l2[:, halves[h]]))
+            nc.vector.tensor_tensor(lead[h][:], a[:].indirect(l1[:, halves[h]]), b_picked[:], SUB)
+
+        nc.scalar.activation(f1[:].indirect(l3[:]), lead[0][:], COPY)
+        nc.scalar.activation(f2[:].indirect(l4[:]), lead[1][:], COPY)
+
+        aa = sb.tile([P, T], F32)
+        bb = sb.tile([P, T], F32)
+        aa_picked = sb.tile([P, I], F32)
+        bb_picked = [sb.tile([P, J], F32, name="bb_picked%d" % h) for h in range(2)]
+        nc.vector.tensor_tensor(aa[:], a[:], f1[:], ADD)
+        nc.scalar.activation(aa_picked[:], aa[:].indirect(l1[:]), COPY)
+        nc.vector.tensor_tensor(bb[:], b[:], f2[:], SUB)
+        nc.vector.tensor_copy(out=bb_picked[0][:], in_=bb[:].indirect(l5[:, halves[0]]))
+        nc.scalar.activation(bb_picked[1][:], bb[:].indirect(l5[:, halves[1]]), COPY)
+        for h in range(2):
+            best = sb.tile([P, J], F32, name="best%d" % h)
+            nc.vector.tensor_tensor(best[:], aa_picked[:, h * J : (h + 1) * J], bb_picked[h][:], MAX)
+            nc.sync.dma_start(out=out[:, h * J : (h + 1) * J], in_=best[:])

@@ -22,6 +22,7 @@ P = 128
 PACK = 4
 N = 256
 HALF = J // 16
+SPLIT = 672
 
 
 def load_scales(nc, plane, scales):
@@ -42,11 +43,11 @@ def spread_scales(nc, plane):
         )
 
 
-def leave_psum(nc, on_vector, dst, bank):
-    if on_vector:
-        nc.vector.tensor_copy(out=dst, in_=bank)
-    else:
-        nc.scalar.copy(out=dst, in_=bank)
+def combine(nc, dst, scores, banks, placed, op):
+    nc.gpsimd.tensor_tensor(dst[:, SPLIT:T], scores[:, SPLIT:T], placed[:, SPLIT:T], op)
+    for first in range(0, SPLIT, N):
+        last = min(first + N, SPLIT)
+        nc.vector.tensor_tensor(dst[:, first:last], banks[first // N][:, 0 : last - first], placed[:, first:last], op)
 
 
 def tile_attend_acceptback_two_kernel(
@@ -83,10 +84,10 @@ def tile_attend_acceptback_two_kernel(
         l5 = sb.tile([P, I // 16], U16)
         nc.sync.dma_start(l5[:], offs5)
 
-        f1 = sb.tile([P, T], F32)
+        f1 = sb.tile([P, T], F32, tag="scores")
         f2 = sb.tile([P, T], F32)
-        nc.vector.memset(f1[:], 0.0)
-        nc.vector.memset(f2[:], 0.0)
+        nc.vector.memset(f1[:].bitcast(I32), 0)
+        nc.vector.memset(f2[:].bitcast(I32), 0)
 
         q_bf = sb.tile([P, Q, PACK], BF16, align_bytes=64)
         nc.vector.tensor_copy(out=q_bf[:], in_=q_raw[:].rearrange("p j w -> p w j"))
@@ -99,6 +100,7 @@ def tile_attend_acceptback_two_kernel(
         spread_scales(nc, c_plane)
 
         a = sb.tile([P, T], F32)
+        a_banks, b_banks = [], []
         b = sb.tile([P, T], F32)
         for c in range(T // N):
             bank = ps.tile([P, N], F32, name="b_bank%d" % c)
@@ -111,7 +113,8 @@ def tile_attend_acceptback_two_kernel(
                 start=True,
                 stop=True,
             )
-            leave_psum(nc, c % 2 == 1, b[:, c * N : (c + 1) * N], bank[:])
+            nc.scalar.copy(out=b[:, c * N : (c + 1) * N], in_=bank[:])
+            b_banks.append(bank)
         for c in range(T // N):
             bank = ps.tile([P, N], F32, name="a_bank%d" % c)
             nc.tensor.matmul_mx(
@@ -123,28 +126,30 @@ def tile_attend_acceptback_two_kernel(
                 start=True,
                 stop=True,
             )
-            leave_psum(nc, c == 2, a[:, c * N : (c + 1) * N], bank[:])
+            nc.scalar.copy(out=a[:, c * N : (c + 1) * N], in_=bank[:])
+            a_banks.append(bank)
 
         halves = [slice(h * HALF, (h + 1) * HALF) for h in range(2)]
         lead = [sb.tile([P, J], F32, name="lead%d" % h) for h in range(2)]
         for h in range(2):
-            b_picked = sb.tile([P, J], F32)
+            b_picked = sb.tile([P, J], F32, tag="picked")
             nc.vector.tensor_copy(out=b_picked[:], in_=b[:].indirect(l2[:, halves[h]]))
             nc.vector.tensor_tensor(lead[h][:], a[:].indirect(l1[:, halves[h]]), b_picked[:], SUB)
 
         nc.scalar.activation(f1[:].indirect(l3[:]), lead[0][:], COPY)
         nc.scalar.activation(f2[:].indirect(l4[:]), lead[1][:], COPY)
 
-        aa = sb.tile([P, T], F32)
-        bb = sb.tile([P, T], F32)
-        aa_picked = sb.tile([P, I], F32)
+        aa = sb.tile([P, T], F32, tag="picked")
+        bb = sb.tile([P, T], F32, tag="scores")
+        aa_picked = [sb.tile([P, J], F32, name="aa_picked%d" % h) for h in range(2)]
         bb_picked = [sb.tile([P, J], F32, name="bb_picked%d" % h) for h in range(2)]
-        nc.vector.tensor_tensor(aa[:], a[:], f1[:], ADD)
-        nc.scalar.activation(aa_picked[:], aa[:].indirect(l1[:]), COPY)
-        nc.vector.tensor_tensor(bb[:], b[:], f2[:], SUB)
+        combine(nc, aa, a, a_banks, f1, ADD)
+        nc.vector.tensor_copy(out=aa_picked[0][:], in_=aa[:].indirect(l1[:, halves[0]]))
+        nc.scalar.activation(aa_picked[1][:], aa[:].indirect(l1[:, halves[1]]), COPY)
+        combine(nc, bb, b, b_banks, f2, SUB)
         nc.vector.tensor_copy(out=bb_picked[0][:], in_=bb[:].indirect(l5[:, halves[0]]))
         nc.scalar.activation(bb_picked[1][:], bb[:].indirect(l5[:, halves[1]]), COPY)
         for h in range(2):
             best = sb.tile([P, J], F32, name="best%d" % h)
-            nc.vector.tensor_tensor(best[:], aa_picked[:, h * J : (h + 1) * J], bb_picked[h][:], MAX)
+            nc.vector.tensor_tensor(best[:], aa_picked[h][:], bb_picked[h][:], MAX)
             nc.sync.dma_start(out=out[:, h * J : (h + 1) * J], in_=best[:])

@@ -22,7 +22,7 @@ P = 128
 PACK = 4
 N = 256
 HALF = J // 16
-SPLIT = 672
+SPLIT = 704
 
 
 def load_scales(nc, plane, scales):
@@ -69,7 +69,7 @@ def tile_attend_acceptback_two_kernel(
         c_src = cache_words[0].rearrange("p n t -> p (n t)").bitcast(I32)
         c_codes = []
         for h in range(2):
-            part = sb.tile([P, T // 2], I32, align_bytes=64, name="c_codes%d" % h)
+            part = sb.tile([P, T // 2], I32, align_bytes=64, name="c_codes%d" % h, tag="late" if h else "early")
             nc.sync.dma_start(out=part[:], in_=c_src[:, h * (T // 2) : (h + 1) * (T // 2)])
             c_codes.append(part)
 
@@ -84,13 +84,15 @@ def tile_attend_acceptback_two_kernel(
         l5 = sb.tile([P, I // 16], U16)
         nc.sync.dma_start(l5[:], offs5)
 
-        f1 = sb.tile([P, T], F32, tag="scores")
+        f1 = sb.tile([P, T], F32)
         f2 = sb.tile([P, T], F32)
         nc.vector.memset(f1[:].bitcast(I32), 0)
         nc.vector.memset(f2[:].bitcast(I32), 0)
 
         q_bf = sb.tile([P, Q, PACK], BF16, align_bytes=64)
-        nc.vector.tensor_copy(out=q_bf[:], in_=q_raw[:].rearrange("p j w -> p w j"))
+        q_turned = q_raw[:].rearrange("p j w -> p w j")
+        nc.vector.tensor_copy(out=q_bf[:, 0 : Q // 2, :], in_=q_turned[:, 0 : Q // 2, :])
+        nc.scalar.copy(out=q_bf[:, Q // 2 : Q, :], in_=q_turned[:, Q // 2 : Q, :])
         spread_scales(nc, d_plane)
         q_codes = sb.tile([P, Q], U32, align_bytes=64)
         q_plane = sb.tile([P, Q], U8, align_bytes=64)
@@ -100,7 +102,7 @@ def tile_attend_acceptback_two_kernel(
         spread_scales(nc, c_plane)
 
         a = sb.tile([P, T], F32)
-        a_banks, b_banks = [], []
+        b_banks = []
         b = sb.tile([P, T], F32)
         for c in range(T // N):
             bank = ps.tile([P, N], F32, name="b_bank%d" % c)
@@ -127,29 +129,29 @@ def tile_attend_acceptback_two_kernel(
                 stop=True,
             )
             nc.scalar.copy(out=a[:, c * N : (c + 1) * N], in_=bank[:])
-            a_banks.append(bank)
 
         halves = [slice(h * HALF, (h + 1) * HALF) for h in range(2)]
         lead = [sb.tile([P, J], F32, name="lead%d" % h) for h in range(2)]
-        for h in range(2):
-            b_picked = sb.tile([P, J], F32, tag="picked")
-            nc.vector.tensor_copy(out=b_picked[:], in_=b[:].indirect(l2[:, halves[h]]))
-            nc.vector.tensor_tensor(lead[h][:], a[:].indirect(l1[:, halves[h]]), b_picked[:], SUB)
+        b_first = sb.tile([P, J], F32)
+        b_second = sb.tile([P, J], F32, align_bytes=64, tag="late")
+        nc.vector.tensor_copy(out=b_first[:], in_=b[:].indirect(l2[:, halves[0]]))
+        nc.scalar.activation(b_second[:], b[:].indirect(l2[:, halves[1]]), COPY)
+        nc.vector.tensor_tensor(lead[0][:], a[:].indirect(l1[:, halves[0]]), b_first[:], SUB)
+        nc.vector.tensor_tensor(lead[1][:], a[:].indirect(l1[:, halves[1]]), b_second[:], SUB)
 
         nc.scalar.activation(f1[:].indirect(l3[:]), lead[0][:], COPY)
         nc.scalar.activation(f2[:].indirect(l4[:]), lead[1][:], COPY)
 
-        aa = sb.tile([P, T], F32, tag="picked")
-        bb = sb.tile([P, T], F32, tag="scores")
-        aa_picked = [sb.tile([P, J], F32, name="aa_picked%d" % h) for h in range(2)]
+        aa = sb.tile([P, T], F32, align_bytes=64, tag="late")
+        bb = sb.tile([P, T], F32)
+        aa_picked = sb.tile([P, I], F32)
         bb_picked = [sb.tile([P, J], F32, name="bb_picked%d" % h) for h in range(2)]
-        combine(nc, aa, a, a_banks, f1, ADD)
-        nc.vector.tensor_copy(out=aa_picked[0][:], in_=aa[:].indirect(l1[:, halves[0]]))
-        nc.scalar.activation(aa_picked[1][:], aa[:].indirect(l1[:, halves[1]]), COPY)
+        nc.vector.tensor_tensor(aa[:], a[:], f1[:], ADD)
+        nc.scalar.activation(aa_picked[:], aa[:].indirect(l1[:]), COPY)
         combine(nc, bb, b, b_banks, f2, SUB)
         nc.vector.tensor_copy(out=bb_picked[0][:], in_=bb[:].indirect(l5[:, halves[0]]))
         nc.scalar.activation(bb_picked[1][:], bb[:].indirect(l5[:, halves[1]]), COPY)
         for h in range(2):
             best = sb.tile([P, J], F32, name="best%d" % h)
-            nc.vector.tensor_tensor(best[:], aa_picked[h][:], bb_picked[h][:], MAX)
+            nc.vector.tensor_tensor(best[:], aa_picked[:, h * J : (h + 1) * J], bb_picked[h][:], MAX)
             nc.sync.dma_start(out=out[:, h * J : (h + 1) * J], in_=best[:])

@@ -59,19 +59,21 @@ def tile_attend_acceptback_two_kernel(
         ps = ctx.enter_context(tc.psum_pool(name="ps", bufs=1))
 
         d_plane = sb.tile([P, 2 * T], U8, align_bytes=64)
-        c_plane = sb.tile([P, 2 * T], U8, align_bytes=64)
+        c_plane = sb.tile([P, N], U8, align_bytes=64)
         q_raw = sb.tile([P, PACK, Q], F32)
         nc.sync.dma_start(out=q_raw[:], in_=query.rearrange("(p j) w -> p j w", j=PACK))
         load_scales(nc, d_plane, draft_scales)
         d_codes = sb.tile([P, 2 * T], U8, align_bytes=64)
         nc.sync.dma_start(out=d_codes[:].bitcast(I32), in_=draft_words[0].bitcast(I32))
-        load_scales(nc, c_plane, cache_scales)
-        c_src = cache_words[0].rearrange("p n t -> p (n t)").bitcast(I32)
-        c_codes = []
-        for h in range(2):
-            part = sb.tile([P, T // 2], I32, align_bytes=64, name="c_codes%d" % h, tag="late" if h else "early")
-            nc.sync.dma_start(out=part[:], in_=c_src[:, h * (T // 2) : (h + 1) * (T // 2)])
-            c_codes.append(part)
+        c_rows = cache_scales[0].bitcast(I32)
+        c_codes = sb.tile([P, T], I32, align_bytes=64, tag="late")
+        for quad in range(4):
+            if quad == 3:
+                nc.sync.dma_start(out=c_codes[:], in_=cache_words[0].rearrange("p n t -> p (n t)").bitcast(I32))
+            nc.sync.dma_start(
+                out=c_plane[:].bitcast(I32)[32 * quad : 32 * quad + 16, :],
+                in_=c_rows[4 * quad : 4 * quad + 4, :].rearrange("r (s c) -> s r c", s=4),
+            )
 
         l2 = sb.tile([P, I // 16], U16)
         nc.sync.dma_start(l2[:], offs2)
@@ -99,7 +101,6 @@ def tile_attend_acceptback_two_kernel(
         nc.vector.quantize_mx(
             out=q_codes[:].bitcast(FP8X4), scales=q_plane[:], in_=q_bf[:].rearrange("p w j -> p (w j)")
         )
-        spread_scales(nc, c_plane)
 
         a = sb.tile([P, T], F32)
         b_banks = []
@@ -123,8 +124,8 @@ def tile_attend_acceptback_two_kernel(
                 out=bank[:],
                 lhsT=q_codes[:].bitcast(FP8X4),
                 lhsT_scale=q_plane[:],
-                rhs=c_codes[c // 2][:, (c % 2) * N : (c % 2 + 1) * N].bitcast(FP8X4),
-                rhs_scale=c_plane[:, c * N : (c + 1) * N],
+                rhs=c_codes[:, c * N : (c + 1) * N].bitcast(FP8X4),
+                rhs_scale=c_plane[4 * c : P, :],
                 start=True,
                 stop=True,
             )
@@ -143,7 +144,7 @@ def tile_attend_acceptback_two_kernel(
         nc.scalar.activation(f2[:].indirect(l4[:]), lead[1][:], COPY)
 
         aa = sb.tile([P, T], F32, align_bytes=64, tag="late")
-        bb = sb.tile([P, T], F32)
+        bb = sb.tile([P, T], F32, tag="bb")
         aa_picked = sb.tile([P, I], F32)
         bb_picked = [sb.tile([P, J], F32, name="bb_picked%d" % h) for h in range(2)]
         nc.vector.tensor_tensor(aa[:], a[:], f1[:], ADD)
@@ -151,7 +152,7 @@ def tile_attend_acceptback_two_kernel(
         combine(nc, bb, b, b_banks, f2, SUB)
         nc.vector.tensor_copy(out=bb_picked[0][:], in_=bb[:].indirect(l5[:, halves[0]]))
         nc.scalar.activation(bb_picked[1][:], bb[:].indirect(l5[:, halves[1]]), COPY)
-        for h in range(2):
-            best = sb.tile([P, J], F32, name="best%d" % h)
+        for h in (1, 0):
+            best = sb.tile([P, J], F32, name="best%d" % h, tag="best" if h else "bb")
             nc.vector.tensor_tensor(best[:], aa_picked[:, h * J : (h + 1) * J], bb_picked[h][:], MAX)
             nc.sync.dma_start(out=out[:, h * J : (h + 1) * J], in_=best[:])

from contextlib import ExitStack

import concourse.mybir as mybir

D, T, I, J, Q = 512, 1024, 512, 256, 128
FLOPS = 2 * 2 * D * T * Q

F32 = mybir.dt.float32
BF16 = mybir.dt.bfloat16
I32 = mybir.dt.int32
U32 = mybir.dt.uint32
U16 = mybir.dt.uint16
U8 = mybir.dt.uint8
FP8X4 = mybir.dt.float8_e4m3fn_x4
FP4X4 = mybir.dt.float4_e2m1fn_x4
ADD = mybir.AluOpType.add
SUB = mybir.AluOpType.subtract
MAX = mybir.AluOpType.max
COPY = mybir.ActivationFunctionType.Copy

P = 128
PACK = 4
N = 256
HALF = J // 16
SPLIT = 704


def load_scales(nc, plane, scales):
    words = plane[:].bitcast(I32)
    rows = scales[0].bitcast(I32)
    for first in (0, 64):
        src = rows[first // 8 : first // 8 + 8, :].rearrange("(s r) c -> r s c", r=4)
        dst = words[first : first + 4, :].rearrange("p (s c) -> p s c", s=2)
        nc.sync.dma_start(out=dst, in_=src)


def spread_scales(nc, plane):
    words = plane[:].bitcast(I32)
    for first in (0, 64):
        nc.vector.tensor_copy(
            out=words[first + 32 : first + 36, 0 : T // 4],
            in_=words[first : first + 4, T // 4 : T // 2],
        )


def combine(nc, dst, scores, banks, placed, op):
    nc.gpsimd.tensor_tensor(dst[:, SPLIT:T], scores[:, SPLIT:T], placed[:, SPLIT:T], op)
    for first in range(0, SPLIT, N):
        last = min(first + N, SPLIT)
        nc.vector.tensor_tensor(dst[:, first:last], banks[first // N][:, 0 : last - first], placed[:, first:last], op)


def tile_attend_acceptback_two_kernel(
    tc, query, cache_words, cache_scales, draft_words, draft_scales, offs, offs2, offs3, offs4, offs5, out
):
    nc = tc.nc
    with ExitStack() as ctx:
        sb = ctx.enter_context(tc.tile_pool(name="sb", bufs=1))
        ps = ctx.enter_context(tc.psum_pool(name="ps", bufs=1))

        d_plane = sb.tile([P, 2 * T], U8, align_bytes=64)
        c_plane = sb.tile([P, N], U8, align_bytes=64)
        q_raw = sb.tile([P, PACK, Q], F32)
        nc.sync.dma_start(out=q_raw[:], in_=query.rearrange("(p j) w -> p j w", j=PACK))
        load_scales(nc, d_plane, draft_scales)
        d_codes = sb.tile([P, 2 * T], U8, align_bytes=64)
        nc.sync.dma_start(out=d_codes[:].bitcast(I32), in_=draft_words[0].bitcast(I32))
        c_rows = cache_scales[0].bitcast(I32)
        c_codes = sb.tile([P, T], I32, align_bytes=64, tag="late")
        for quad in range(4):
            if quad == 3:
                nc.sync.dma_start(out=c_codes[:], in_=cache_words[0].rearrange("p n t -> p (n t)").bitcast(I32))
            nc.sync.dma_start(
                out=c_plane[:].bitcast(I32)[32 * quad : 32 * quad + 16, :],
                in_=c_rows[4 * quad : 4 * quad + 4, :].rearrange("r (s c) -> s r c", s=4),
            )

        l2 = sb.tile([P, I // 16], U16)
        nc.sync.dma_start(l2[:], offs2)
        l1 = sb.tile([P, I // 16], U16)
        nc.sync.dma_start(l1[:], offs)
        l3 = sb.tile([P, J // 16], U16)
        nc.sync.dma_start(l3[:], offs3)
        l4 = sb.tile([P, J // 16], U16)
        nc.sync.dma_start(l4[:], offs4)
        l5 = sb.tile([P, I // 16], U16)
        nc.sync.dma_start(l5[:], offs5)

        f1 = sb.tile([P, T], F32)
        f2 = sb.tile([P, T], F32)
        nc.vector.memset(f1[:].bitcast(I32), 0)
        nc.vector.memset(f2[:].bitcast(I32), 0)

        q_bf = sb.tile([P, Q, PACK], BF16, align_bytes=64)
        q_turned = q_raw[:].rearrange("p j w -> p w j")
        nc.vector.tensor_copy(out=q_bf[:, 0 : Q // 2, :], in_=q_turned[:, 0 : Q // 2, :])
        nc.scalar.copy(out=q_bf[:, Q // 2 : Q, :], in_=q_turned[:, Q // 2 : Q, :])
        spread_scales(nc, d_plane)
        q_codes = sb.tile([P, Q], U32, align_bytes=64)
        q_plane = sb.tile([P, Q], U8, align_bytes=64)
        nc.vector.quantize_mx(
            out=q_codes[:].bitcast(FP8X4), scales=q_plane[:], in_=q_bf[:].rearrange("p w j -> p (w j)")
        )

        a = sb.tile([P, T], F32)
        b_banks = []
        b = sb.tile([P, T], F32)
        for c in range(T // N):
            bank = ps.tile([P, N], F32, name="b_bank%d" % c)
            nc.tensor.matmul_mx(
                out=bank[:],
                lhsT=q_codes[:].bitcast(FP8X4),
                lhsT_scale=q_plane[:],
                rhs=d_codes[:, 2 * c * N : 2 * (c + 1) * N].bitcast(FP4X4),
                rhs_scale=d_plane[:, c * N : (c + 1) * N],
                start=True,
                stop=True,
            )
            nc.scalar.copy(out=b[:, c * N : (c + 1) * N], in_=bank[:])
            b_banks.append(bank)
        for c in range(T // N):
            bank = ps.tile([P, N], F32, name="a_bank%d" % c)
            nc.tensor.matmul_mx(
                out=bank[:],
                lhsT=q_codes[:].bitcast(FP8X4),
                lhsT_scale=q_plane[:],
                rhs=c_codes[:, c * N : (c + 1) * N].bitcast(FP8X4),
                rhs_scale=c_plane[4 * c : P, :],
                start=True,
                stop=True,
            )
            nc.scalar.copy(out=a[:, c * N : (c + 1) * N], in_=bank[:])

        halves = [slice(h * HALF, (h + 1) * HALF) for h in range(2)]
        lead = [sb.tile([P, J], F32, name="lead%d" % h) for h in range(2)]
        b_first = sb.tile([P, J], F32)
        b_second = sb.tile([P, J], F32, align_bytes=64, tag="late")
        nc.vector.tensor_copy(out=b_first[:], in_=b[:].indirect(l2[:, halves[0]]))
        nc.scalar.activation(b_second[:], b[:].indirect(l2[:, halves[1]]), COPY)
        nc.vector.tensor_tensor(lead[0][:], a[:].indirect(l1[:, halves[0]]), b_first[:], SUB)
        nc.vector.tensor_tensor(lead[1][:], a[:].indirect(l1[:, halves[1]]), b_second[:], SUB)

        nc.scalar.activation(f1[:].indirect(l3[:]), lead[0][:], COPY)
        nc.scalar.activation(f2[:].indirect(l4[:]), lead[1][:], COPY)

        aa = sb.tile([P, T], F32, align_bytes=64, tag="late")
        bb = sb.tile([P, T], F32, tag="bb")
        aa_picked = sb.tile([P, I], F32)
        bb_picked = [sb.tile([P, J], F32, name="bb_picked%d" % h) for h in range(2)]
        nc.vector.tensor_tensor(aa[:], a[:], f1[:], ADD)
        nc.scalar.activation(aa_picked[:], aa[:].indirect(l1[:]), COPY)
        combine(nc, bb, b, b_banks, f2, SUB)
        nc.vector.tensor_copy(out=bb_picked[0][:], in_=bb[:].indirect(l5[:, halves[0]]))
        nc.scalar.activation(bb_picked[1][:], bb[:].indirect(l5[:, halves[1]]), COPY)
        for h in (1, 0):
            best = sb.tile([P, J], F32, name="best%d" % h, tag="best" if h else "bb")
            nc.vector.tensor_tensor(best[:], aa_picked[:, h * J : (h + 1) * J], bb_picked[h][:], MAX)
            nc.sync.dma_start(out=out[:, h * J : (h + 1) * J], in_=best[:])
